import numpy as np
import ml_dtypes


def mxq(x, axis, fmt="e4m3"):
    dtype, down = {"e4m3": (ml_dtypes.float8_e4m3fn, 7), "e5m2": (ml_dtypes.float8_e5m2, 14)}[fmt]
    v = np.moveaxis(np.asarray(x, np.float32).astype(ml_dtypes.bfloat16).astype(np.float64), axis, -1)
    blocks = v.reshape(v.shape[:-1] + (-1, 32))
    amax = np.abs(blocks).max(-1, keepdims=True)
    byte = np.maximum(np.where(amax > 0, np.frexp(amax)[1] - 1 + 127, 0) - down, 1)
    scale = np.exp2(byte - 127.0)
    codes = (blocks / scale).astype(np.float32).astype(dtype).astype(np.float64)
    return np.moveaxis((codes * scale).reshape(v.shape), -1, axis)


WIDE = False


def mx_kscale(k):
    if not WIDE:
        return np.ones(k)
    levels = np.array([10, -10, 5, -5, 0])
    if k % 512:
        return np.exp2(np.random.permutation(np.resize(levels, k // 32))).repeat(32)
    a = np.empty((k // 512, 16))
    for p in range(k // 512):
        a[p, :8] = np.random.permutation(np.resize(levels, 8))
        for g in range(8):
            far = levels[np.abs(levels - a[p, g]) >= 10]
            a[p, g + 8] = far[np.random.randint(len(far))]
    return np.exp2(a.ravel()).repeat(32)


def f64(x):
    return np.asarray(x).astype(np.float64)


def striped(idx):
    return np.tile(idx.reshape(-1, 16).T, (8, 1)).astype(np.uint16)


def unstriped(offs):
    return offs[:16].T.reshape(-1).astype(np.int64)


E2M1 = np.array([0.0, 0.5, 1.0, 1.5, 2.0, 3.0, 4.0, 6.0, -0.0, -0.5, -1.0, -1.5, -2.0, -3.0, -4.0, -6.0])


def pack_weight(w, fmt):
    k, n = w.shape
    w = f64(np.asarray(w, np.float32).astype(ml_dtypes.bfloat16)).reshape(k // 32, 32, n)
    amax = np.abs(w).max(1)
    if fmt == "e4m3":
        byte = np.frexp(amax)[1] - 1 + 127 - 7
    else:
        mant, ex = np.frexp(amax / 6.0)
        byte = np.where(mant > 0.5, ex, ex - 1) + 127
    byte = np.clip(np.where(amax > 0, byte, 1), 1, 254)
    scaled = (w * np.exp2(127.0 - byte)[:, None, :]).reshape(k, n).astype(np.float32)
    by_word = np.ascontiguousarray(scaled.reshape(k // 512, 128, 4, n).transpose(0, 1, 3, 2))
    if fmt == "e4m3":
        words = by_word.astype(ml_dtypes.float8_e4m3fn).view(np.uint8)
    else:
        c = by_word.astype(ml_dtypes.float4_e2m1fn).view(np.uint8) & 0xF
        words = (c[..., 0::2] | (c[..., 1::2] << 4)).reshape(k // 512, 128, 2 * n)
    return np.ascontiguousarray(words), np.ascontiguousarray(byte.astype(np.uint8).reshape(k // 512, 16, n))


def unpack_weight(words, scales, fmt):
    g, _, n = scales.shape
    words = np.ascontiguousarray(words).reshape(g, 128, n, -1)
    if fmt == "e4m3":
        vals = words.view(ml_dtypes.float8_e4m3fn).astype(np.float64)
    else:
        nib = np.empty((g, 128, n, 4), np.uint8)
        nib[..., 0::2] = words & 0xF
        nib[..., 1::2] = words >> 4
        vals = E2M1[nib]
    vals = vals * np.repeat(np.exp2(scales.astype(np.float64) - 127.0), 8, axis=1)[..., None]
    return vals.transpose(0, 1, 3, 2).reshape(g * 512, n)


def relu(v):
    return np.maximum(v, 0.0)


K, T, E, C, D, H, N = 512, 1024, 4, 256, 128, 512, 256


def by_expert(wq, xq, C):
    return np.concatenate([wq[e].T @ xq[:, e * C:(e + 1) * C] for e in range(E)], axis=1)


def setup_inputs():
    n = np.random.standard_normal
    s = mx_kscale(K)
    u = mx_kscale(H)
    first = np.random.permutation(np.repeat(np.arange(E), C))
    slots1 = np.concatenate([np.random.permutation(np.flatnonzero(first == e)) for e in range(E)])
    free = np.ones(T, bool); slots2 = np.empty(E * D, np.int64)
    for e in np.random.permutation(E):
        pick = np.random.permutation(np.flatnonzero(free & (first != e)))[:D]; slots2[e * D:(e + 1) * D] = pick; free[pick] = False
    g1 = np.random.uniform(0.5, 1.0, T); g2 = 1.0 - g1
    x = pack_weight(n((K, T)) * s[:, None], "e4m3")
    w1 = [pack_weight(m, "e4m3") for m in n((E, K, H)) / np.sqrt(K) / s[None, :, None] * u]
    w2 = [pack_weight(m, "e4m3") for m in n((E, H, N)) / np.sqrt(H) / u[None, :, None]]
    return {
        "x_words": x[0],
        "x_scales": x[1],
        "w1_words": np.stack([m[0] for m in w1]),
        "w1_scales": np.stack([m[1] for m in w1]),
        "w2_words": np.stack([m[0] for m in w2]),
        "w2_scales": np.stack([m[1] for m in w2]),
        "gate1": (np.tile(g1[slots1], (128, 1))).astype(np.float32),
        "gate2": (np.tile(g2[slots2], (128, 1))).astype(np.float32),
        "offs": striped(slots1),
        "offs2": striped(slots2),
    }


def reference(x_words, x_scales, w1_words, w1_scales, w2_words, w2_scales, gate1, gate2, offs, offs2):
    w1 = np.stack([unpack_weight(w1_words[e], w1_scales[e], "e4m3") for e in range(E)])
    w2 = np.stack([unpack_weight(w2_words[e], w2_scales[e], "e4m3") for e in range(E)])
    idx, idx2 = unstriped(offs), unstriped(offs2)
    x = unpack_weight(x_words, x_scales, "e4m3")
    h = relu(by_expert(w1, x[:, idx], C))
    y = by_expert(w2, mxq(h, 0, "e4m3"), C)
    h = relu(by_expert(w1, x[:, idx2], D))
    z = by_expert(w2, mxq(h, 0, "e4m3"), D)
    out = np.zeros((N, T))
    out[:, idx] = f64(gate1[:1]) * y
    out[:, idx2] += f64(gate2[:1]) * z
    return out

@@ -1,0 +1,208 @@
+from contextlib import ExitStack
+
+import concourse.mybir as mybir
+from concourse.masks import make_identity
+
+K, T, E, C, D, H, N = 512, 1024, 4, 256, 128, 512, 256
+FLOPS = 2 * (E * C + E * D) * (K * H + H * N)
+
+F32 = mybir.dt.float32
+BF16 = mybir.dt.bfloat16
+I32 = mybir.dt.int32
+U32 = mybir.dt.uint32
+U16 = mybir.dt.uint16
+U8 = mybir.dt.uint8
+FP8X4 = mybir.dt.float8_e4m3fn_x4
+RELU = mybir.ActivationFunctionType.Relu
+MULT = mybir.AluOpType.mult
+ADD = mybir.AluOpType.add
+
+P = 128
+U = 256
+FUSED = False
+
+
+def tile_moe_ada_mlp_relu_kernel(
+    tc, x_words, x_scales, w1_words, w1_scales, w2_words, w2_scales, gate1, gate2, offs, offs2, out
+):
+    nc = tc.nc
+    with ExitStack() as ctx:
+        keep = ctx.enter_context(tc.tile_pool(name="keep", bufs=1))
+        ring = ctx.enter_context(tc.tile_pool(name="ring", bufs=3))
+        psum = ctx.enter_context(tc.psum_pool(name="psum", bufs=1))
+
+        list1 = keep.tile([P, T // 16], U16, name="list1")
+        list2 = keep.tile([P, E * D // 16], U16, name="list2")
+        xs = keep.tile([P, T], U8, name="xs", align_bytes=64)
+        xw = keep.tile([P, T], I32, name="xw", align_bytes=64)
+        w1s = keep.tile([P, H], U8, name="w1s", align_bytes=64)
+        w2s = keep.tile([P, N], U8, name="w2s", align_bytes=64)
+        w1 = [keep.tile([P, H], I32, name="w1_%d" % e, align_bytes=64) for e in range(E)]
+        w2 = keep.tile([P, E, N], I32, name="w2", align_bytes=64)
+        g1 = keep.tile([P, E * C], F32, name="g1")
+        g2 = keep.tile([P, E * D], F32, name="g2")
+        ident = keep.tile([P, P], F32, name="ident")
+        first = [keep.tile([P, T], F32, name="first%d" % a) for a in range(2)]
+        second = [keep.tile([P, T], F32, name="second%d" % a) for a in range(2)]
+        total = [keep.tile([P, T], F32, name="total%d" % a) for a in range(2)]
+
+        nc.vector.memset(xs[:].bitcast(I32), 0)
+        nc.vector.memset(w1s[:].bitcast(I32), 0)
+        nc.vector.memset(w2s[:].bitcast(I32), 0)
+        nc.sync.dma_start(list1[:], offs)
+        for q in range(4):
+            nc.sync.dma_start(xs[32 * q : 32 * q + 4, :].bitcast(I32), x_scales[0, 4 * q : 4 * q + 4, :].bitcast(I32))
+        nc.sync.dma_start(xw[:], x_words[0].rearrange("p t d -> p (t d)").bitcast(I32))
+        make_identity(nc, ident[:])
+        for q in range(4):
+            nc.gpsimd.dma_start(w2s[32 * q : 32 * q + 16, :].bitcast(I32), w2_scales[:, 0, 4 * q : 4 * q + 4, :].bitcast(I32))
+
+        def load_w1(e):
+            nc.sync.dma_start(w1[e][:], w1_words[e, 0].rearrange("p i d -> p (i d)").bitcast(I32))
+
+        load_w1(0)
+        for q in range(4):
+            nc.sync.dma_start(w1s[32 * q : 32 * q + 16, :].bitcast(I32), w1_scales[:, 0, 4 * q : 4 * q + 4, :].bitcast(I32))
+        load_w1(1)
+        nc.sync.dma_start(list2[:], offs2)
+        nc.sync.dma_start(w2[:], w2_words[:, 0].rearrange("e p n d -> p e (n d)").bitcast(I32))
+        nc.sync.dma_start(g1[:], gate1)
+        load_w1(2)
+        load_w1(3)
+        nc.sync.dma_start(g2[:], gate2)
+        for a in range(2):
+            nc.vector.memset(second[a][:], 0.0)
+
+        units = [
+            (list1, g1, first, 0, (0, 0)),
+            (list1, g1, first, 256, (1, 1)),
+            (list2, g2, second, 0, (0, 1)),
+            (list1, g1, first, 512, (2, 2)),
+            (list1, g1, first, 768, (3, 3)),
+            (list2, g2, second, 256, (2, 3)),
+        ]
+        gw = [keep.tile([P, U], I32, name="gw%d" % u, align_bytes=64) for u in range(6)]
+        gs = [keep.tile([P, U], U8, name="gs%d" % u, align_bytes=64) for u in range(6)]
+        ysb = [keep.tile([P, 2, U], F32, name="ysb%d" % u) for u in range(6)]
+
+        def offsets(u):
+            lst, s0 = units[u][0], units[u][3]
+            return lst[:, s0 // 16 : (s0 + U) // 16]
+
+        def gather_scales(u):
+            nc.vector.tensor_copy(gs[u][:], xs[:].indirect(offsets(u)))
+
+        def gather_words(u):
+            nc.vector.tensor_copy(gw[u][:].bitcast(U32), xw[:].bitcast(U32).indirect(offsets(u)))
+
+        hin = {}
+
+        def layer1(u):
+            experts = units[u][4]
+            turned = psum.tile([P, 2, 2, P], F32, name="turned", bufs=2)
+            for b in range(2):
+                e = experts[b]
+                cols = slice(b * P, (b + 1) * P)
+                acc = psum.tile([P, H], F32, name="acc1", bufs=4)
+                nc.tensor.matmul_mx(
+                    out=acc[:], lhsT=gw[u][:, cols].bitcast(FP8X4), lhsT_scale=gs[u][:, cols],
+                    rhs=w1[e][:].bitcast(FP8X4), rhs_scale=w1s[4 * e : P, :], start=True, stop=True,
+                )
+                hb = ring.tile([P, H], BF16, name="hb", bufs=4)
+                nc.scalar.activation(
+                    hb[:].rearrange("s (v p d) -> s v p d", v=2, d=2),
+                    acc[:].rearrange("s (p v d) -> s v p d", v=2, d=2),
+                    RELU,
+                )
+                for v in range(2):
+                    nc.tensor.transpose(turned[:, b, v, :], hb[:].bitcast(F32)[:, v * P : (v + 1) * P], ident[:])
+            hin[u] = ring.tile([P, 4 * U], BF16, name="hin", align_bytes=64)
+            nc.scalar.copy(
+                hin[u][:].bitcast(F32).rearrange("p (b s v) -> p b s v", b=2, v=2),
+                turned[:].rearrange("p b v s -> p b s v"),
+            )
+
+        hq = {}
+
+        def quantize(u):
+            words = ring.tile([P, U], U32, name="hw", align_bytes=64)
+            scales = ring.tile([P, U], U8, name="hs", align_bytes=64)
+            nc.vector.quantize_mx(out=words[:].bitcast(FP8X4), scales=scales[:], in_=hin[u][:])
+            hq[u] = (words, scales)
+
+        def layer2(u):
+            experts = units[u][4]
+            words, scales = hq[u]
+            acc = psum.tile([P, 2, U], F32, name="acc2", bufs=2)
+            runs = [(experts[0], slice(0, U))] if experts[0] == experts[1] else [(experts[b], slice(b * P, (b + 1) * P)) for b in range(2)]
+            for a in range(2):
+                ncols = slice(a * P, (a + 1) * P)
+                for e, cols in runs:
+                    nc.tensor.matmul_mx(
+                        out=acc[:, a, cols], lhsT=w2[:, e, ncols].bitcast(FP8X4), lhsT_scale=w2s[4 * e : P, ncols],
+                        rhs=words[:, cols].bitcast(FP8X4), rhs_scale=scales[:, cols], start=True, stop=True,
+                    )
+            gate, s0 = units[u][1], units[u][3]
+            if FUSED:
+                nc.scalar.copy(ysb[u][:], acc[:])
+            else:
+                nc.vector.tensor_tensor(ysb[u][:], acc[:], gate[:, s0 : s0 + U].unsqueeze(1).to_broadcast([P, 2, U]), MULT)
+
+        def scatter(u, a):
+            gate, windows, s0 = units[u][1], units[u][2], units[u][3]
+            if FUSED:
+                nc.vector.tensor_tensor(windows[a][:].indirect(offsets(u)), ysb[u][:, a, :], gate[:, s0 : s0 + U], MULT)
+            else:
+                nc.vector.tensor_copy(windows[a][:].indirect(offsets(u)), ysb[u][:, a, :])
+
+        def finish(a, pieces):
+            w = T // pieces
+            for j in range(pieces):
+                cols = slice(j * w, (j + 1) * w)
+                nc.vector.tensor_tensor(total[a][:, cols], first[a][:, cols], second[a][:, cols], ADD)
+                nc.sync.dma_start(out[a * P : (a + 1) * P, cols], total[a][:, cols])
+
+        gather_scales(0)
+        gather_scales(1)
+        gather_words(0)
+        layer1(0)
+        gather_words(1)
+        layer1(1)
+        gather_scales(2)
+        gather_words(2)
+        quantize(0)
+        layer2(0)
+        layer1(2)
+        gather_scales(3)
+        gather_words(3)
+        quantize(1)
+        layer2(1)
+        layer1(3)
+        gather_scales(4)
+        gather_words(4)
+        gather_scales(5)
+        gather_words(5)
+        scatter(0, 0)
+        quantize(2)
+        layer2(2)
+        layer1(4)
+        scatter(0, 1)
+        scatter(1, 0)
+        quantize(3)
+        layer2(3)
+        layer1(5)
+        scatter(1, 1)
+        scatter(2, 0)
+        quantize(4)
+        layer2(4)
+        scatter(3, 0)
+        quantize(5)
+        layer2(5)
+        scatter(2, 1)
+        scatter(4, 0)
+        scatter(5, 0)
+        scatter(3, 1)
+        finish(0, 1)
+        scatter(4, 1)
+        scatter(5, 1)
+        finish(1, 2)

@@ -19,7 +19,6 @@ ADD = mybir.AluOpType.add
 
 P = 128
 U = 256
-FUSED = False
 
 
 def tile_moe_ada_mlp_relu_kernel(
@@ -31,31 +30,28 @@ def tile_moe_ada_mlp_relu_kernel(
         ring = ctx.enter_context(tc.tile_pool(name="ring", bufs=3))
         psum = ctx.enter_context(tc.psum_pool(name="psum", bufs=1))
 
-        list1 = keep.tile([P, T // 16], U16, name="list1")
-        list2 = keep.tile([P, E * D // 16], U16, name="list2")
+        slots = (E * C, E * D)
+        lists = [keep.tile([P, slots[c] // 16], U16, name="list%d" % c) for c in range(2)]
         xs = keep.tile([P, T], U8, name="xs", align_bytes=64)
         xw = keep.tile([P, T], I32, name="xw", align_bytes=64)
         w1s = keep.tile([P, H], U8, name="w1s", align_bytes=64)
         w2s = keep.tile([P, N], U8, name="w2s", align_bytes=64)
         w1 = [keep.tile([P, H], I32, name="w1_%d" % e, align_bytes=64) for e in range(E)]
         w2 = keep.tile([P, E, N], I32, name="w2", align_bytes=64)
-        g1 = keep.tile([P, E * C], F32, name="g1")
-        g2 = keep.tile([P, E * D], F32, name="g2")
+        gates = [keep.tile([P, slots[c]], F32, name="gate%d" % c) for c in range(2)]
         ident = keep.tile([P, P], F32, name="ident")
-        first = [keep.tile([P, T], F32, name="first%d" % a) for a in range(2)]
-        second = [keep.tile([P, T], F32, name="second%d" % a) for a in range(2)]
+        windows = [[keep.tile([P, T], F32, name="window%d%d" % (c, a)) for a in range(2)] for c in range(2)]
         total = [keep.tile([P, T], F32, name="total%d" % a) for a in range(2)]
+        ysb = [keep.tile([P, 2, slots[c]], F32, name="ysb%d" % c) for c in range(2)]
 
-        nc.vector.memset(xs[:].bitcast(I32), 0)
         nc.vector.memset(w1s[:].bitcast(I32), 0)
         nc.vector.memset(w2s[:].bitcast(I32), 0)
-        nc.sync.dma_start(list1[:], offs)
+        nc.sync.dma_start(lists[0][:], offs)
         for q in range(4):
-            nc.sync.dma_start(xs[32 * q : 32 * q + 4, :].bitcast(I32), x_scales[0, 4 * q : 4 * q + 4, :].bitcast(I32))
+            rows = x_scales[0, 4 * q : 4 * q + 4, :].bitcast(I32)
+            nc.sync.dma_start(xs[32 * q : 32 * q + 32, :].bitcast(I32), rows.unsqueeze(0).to_broadcast([8, 4, T // 4]))
         nc.sync.dma_start(xw[:], x_words[0].rearrange("p t d -> p (t d)").bitcast(I32))
         make_identity(nc, ident[:])
-        for q in range(4):
-            nc.gpsimd.dma_start(w2s[32 * q : 32 * q + 16, :].bitcast(I32), w2_scales[:, 0, 4 * q : 4 * q + 4, :].bitcast(I32))
 
         def load_w1(e):
             nc.sync.dma_start(w1[e][:], w1_words[e, 0].rearrange("p i d -> p (i d)").bitcast(I32))
@@ -63,146 +59,181 @@ def tile_moe_ada_mlp_relu_kernel(
         load_w1(0)
         for q in range(4):
             nc.sync.dma_start(w1s[32 * q : 32 * q + 16, :].bitcast(I32), w1_scales[:, 0, 4 * q : 4 * q + 4, :].bitcast(I32))
+        nc.sync.dma_start(lists[1][:], offs2)
         load_w1(1)
-        nc.sync.dma_start(list2[:], offs2)
+        for q in range(4):
+            nc.sync.dma_start(w2s[32 * q : 32 * q + 16, :].bitcast(I32), w2_scales[:, 0, 4 * q : 4 * q + 4, :].bitcast(I32))
         nc.sync.dma_start(w2[:], w2_words[:, 0].rearrange("e p n d -> p e (n d)").bitcast(I32))
-        nc.sync.dma_start(g1[:], gate1)
+        nc.sync.dma_start(gates[0][:], gate1)
         load_w1(2)
         load_w1(3)
-        nc.sync.dma_start(g2[:], gate2)
+        nc.sync.dma_start(gates[1][:], gate2)
         for a in range(2):
-            nc.vector.memset(second[a][:], 0.0)
+            nc.vector.memset(windows[1][a][:], 0.0)
 
-        units = [
-            (list1, g1, first, 0, (0, 0)),
-            (list1, g1, first, 256, (1, 1)),
-            (list2, g2, second, 0, (0, 1)),
-            (list1, g1, first, 512, (2, 2)),
-            (list1, g1, first, 768, (3, 3)),
-            (list2, g2, second, 256, (2, 3)),
-        ]
-        gw = [keep.tile([P, U], I32, name="gw%d" % u, align_bytes=64) for u in range(6)]
-        gs = [keep.tile([P, U], U8, name="gs%d" % u, align_bytes=64) for u in range(6)]
-        ysb = [keep.tile([P, 2, U], F32, name="ysb%d" % u) for u in range(6)]
+        units = [(0, 0, (0, 0)), (0, 256, (1, 1)), (1, 0, (0, 1)), (0, 512, (2, 2)), (0, 768, (3, 3)), (1, 256, (2, 3))]
 
-        def offsets(u):
-            lst, s0 = units[u][0], units[u][3]
-            return lst[:, s0 // 16 : (s0 + U) // 16]
+        def offsets(c, s0, s1):
+            return lists[c][:, s0 // 16 : s1 // 16]
 
-        def gather_scales(u):
-            nc.vector.tensor_copy(gs[u][:], xs[:].indirect(offsets(u)))
+        gw, gs = {}, {}
 
-        def gather_words(u):
-            nc.vector.tensor_copy(gw[u][:].bitcast(U32), xw[:].bitcast(U32).indirect(offsets(u)))
+        def gather_scales(us, tag):
+            c, s0 = units[us[0]][0], units[us[0]][1]
+            tile = keep.tile([P, U * len(us)], U8, name=tag, align_bytes=64)
+            nc.vector.tensor_copy(tile[:], xs[:].indirect(offsets(c, s0, s0 + U * len(us))))
+            for j, u in enumerate(us):
+                gs[u] = tile[:, j * U : (j + 1) * U]
 
-        hin = {}
+        def gather_words(us, tag):
+            c, s0 = units[us[0]][0], units[us[0]][1]
+            tile = keep.tile([P, U * len(us)], I32, name=tag, align_bytes=64)
+            nc.vector.tensor_copy(tile[:].bitcast(U32), xw[:].bitcast(U32).indirect(offsets(c, s0, s0 + U * len(us))))
+            for j, u in enumerate(us):
+                gw[u] = tile[:, j * U : (j + 1) * U]
 
-        def layer1(u):
-            experts = units[u][4]
-            turned = psum.tile([P, 2, 2, P], F32, name="turned", bufs=2)
-            for b in range(2):
-                e = experts[b]
-                cols = slice(b * P, (b + 1) * P)
-                acc = psum.tile([P, H], F32, name="acc1", bufs=4)
-                nc.tensor.matmul_mx(
-                    out=acc[:], lhsT=gw[u][:, cols].bitcast(FP8X4), lhsT_scale=gs[u][:, cols],
-                    rhs=w1[e][:].bitcast(FP8X4), rhs_scale=w1s[4 * e : P, :], start=True, stop=True,
-                )
-                hb = ring.tile([P, H], BF16, name="hb", bufs=4)
-                nc.scalar.activation(
-                    hb[:].rearrange("s (v p d) -> s v p d", v=2, d=2),
-                    acc[:].rearrange("s (p v d) -> s v p d", v=2, d=2),
-                    RELU,
-                )
-                for v in range(2):
-                    nc.tensor.transpose(turned[:, b, v, :], hb[:].bitcast(F32)[:, v * P : (v + 1) * P], ident[:])
-            hin[u] = ring.tile([P, 4 * U], BF16, name="hin", align_bytes=64)
+        hin, turned = {}, {}
+
+        def block(u, b, bank=None):
+            e = units[u][2][b]
+            if b == 0:
+                turned[u] = psum.tile([P, 2, 2, P], F32, name=bank, bufs=1)
+            cols = slice(b * P, (b + 1) * P)
+            acc = psum.tile([P, H], F32, name="acc1", bufs=4)
+            nc.tensor.matmul_mx(
+                out=acc[:], lhsT=gw[u][:, cols].bitcast(FP8X4), lhsT_scale=gs[u][:, cols],
+                rhs=w1[e][:].bitcast(FP8X4), rhs_scale=w1s[4 * e : P, :], start=True, stop=True,
+            )
+            hb = ring.tile([P, H], BF16, name="hb", bufs=4)
+            nc.scalar.activation(
+                hb[:].rearrange("s (v p d) -> s v p d", v=2, d=2),
+                acc[:].rearrange("s (p v d) -> s v p d", v=2, d=2),
+                RELU,
+            )
+            for v in range(2):
+                nc.tensor.transpose(turned[u][:, b, v, :], hb[:].bitcast(F32)[:, v * P : (v + 1) * P], ident[:])
+
+        def regroup(u):
+            hin[u] = keep.tile([P, 4 * U], BF16, name="hin%d" % u, align_bytes=64)
             nc.scalar.copy(
                 hin[u][:].bitcast(F32).rearrange("p (b s v) -> p b s v", b=2, v=2),
-                turned[:].rearrange("p b v s -> p b s v"),
+                turned[u][:].rearrange("p b v s -> p b s v"),
             )
 
         hq = {}
 
         def quantize(u):
-            words = ring.tile([P, U], U32, name="hw", align_bytes=64)
-            scales = ring.tile([P, U], U8, name="hs", align_bytes=64)
+            words = keep.tile([P, U], U32, name="hw%d" % u, align_bytes=64)
+            scales = keep.tile([P, U], U8, name="hs%d" % u, align_bytes=64)
             nc.vector.quantize_mx(out=words[:].bitcast(FP8X4), scales=scales[:], in_=hin[u][:])
             hq[u] = (words, scales)
 
-        def layer2(u):
-            experts = units[u][4]
+        acc2 = {}
+
+        def layer2(u, halves, bank):
+            experts = units[u][2]
             words, scales = hq[u]
-            acc = psum.tile([P, 2, U], F32, name="acc2", bufs=2)
+            acc = psum.tile([P, 2, U], F32, name=bank, bufs=1)
             runs = [(experts[0], slice(0, U))] if experts[0] == experts[1] else [(experts[b], slice(b * P, (b + 1) * P)) for b in range(2)]
-            for a in range(2):
+            for a in halves:
+                acc2[u, a] = acc
                 ncols = slice(a * P, (a + 1) * P)
                 for e, cols in runs:
                     nc.tensor.matmul_mx(
                         out=acc[:, a, cols], lhsT=w2[:, e, ncols].bitcast(FP8X4), lhsT_scale=w2s[4 * e : P, ncols],
                         rhs=words[:, cols].bitcast(FP8X4), rhs_scale=scales[:, cols], start=True, stop=True,
                     )
-            gate, s0 = units[u][1], units[u][3]
-            if FUSED:
-                nc.scalar.copy(ysb[u][:], acc[:])
-            else:
-                nc.vector.tensor_tensor(ysb[u][:], acc[:], gate[:, s0 : s0 + U].unsqueeze(1).to_broadcast([P, 2, U]), MULT)
 
-        def scatter(u, a):
-            gate, windows, s0 = units[u][1], units[u][2], units[u][3]
-            if FUSED:
-                nc.vector.tensor_tensor(windows[a][:].indirect(offsets(u)), ysb[u][:, a, :], gate[:, s0 : s0 + U], MULT)
-            else:
-                nc.vector.tensor_copy(windows[a][:].indirect(offsets(u)), ysb[u][:, a, :])
+        def evac(u, a0, a1):
+            c, s0 = units[u][0], units[u][1]
+            nc.scalar.copy(ysb[c][:, a0:a1, s0 : s0 + U], acc2[u, a0][:, a0:a1, :])
 
-        def finish(a, pieces):
-            w = T // pieces
-            for j in range(pieces):
-                cols = slice(j * w, (j + 1) * w)
-                nc.vector.tensor_tensor(total[a][:, cols], first[a][:, cols], second[a][:, cols], ADD)
+        def scatter(c, s0, s1, a):
+            nc.vector.tensor_tensor(windows[c][a][:].indirect(offsets(c, s0, s1)), ysb[c][:, a, s0:s1], gates[c][:, s0:s1], MULT)
+
+        def finish(a, cuts):
+            for j in range(len(cuts) - 1):
+                cols = slice(cuts[j], cuts[j + 1])
+                nc.vector.tensor_tensor(total[a][:, cols], windows[0][a][:, cols], windows[1][a][:, cols], ADD)
                 nc.sync.dma_start(out[a * P : (a + 1) * P, cols], total[a][:, cols])
 
-        gather_scales(0)
-        gather_scales(1)
-        gather_words(0)
-        layer1(0)
-        gather_words(1)
-        layer1(1)
-        gather_scales(2)
-        gather_words(2)
+        def finish_on_tensor(a):
+            for half in range(2):
+                summed = psum.tile([P, 4, P], F32, name="acc1", bufs=4)
+                for j in range(4):
+                    cols = slice((4 * half + j) * P, (4 * half + j + 1) * P)
+                    for c in range(2):
+                        nc.tensor.matmul(summed[:, j, :], lhsT=windows[c][a][:, cols], rhs=ident[:], start=(c == 0), stop=(c == 1), is_transpose=True)
+                flipped = ring.tile([P, 4, P], F32, name="flipped")
+                nc.scalar.copy(flipped[:], summed[:])
+                back = psum.tile([P, 4, P], F32, name="acc1", bufs=4)
+                for j in range(4):
+                    nc.tensor.transpose(back[:, j, :], flipped[:, j, :], ident[:])
+                cols = slice(half * 4 * P, (half + 1) * 4 * P)
+                nc.scalar.copy(total[a][:, cols], back[:].rearrange("p j t -> p (j t)"))
+                nc.sync.dma_start(out[a * P : (a + 1) * P, cols], total[a][:, cols])
+
+        gather_scales([0, 1], "gs01")
+        gather_words([0], "gw0")
+        gather_words([1], "gw1")
+        gather_scales([2], "gs2")
+        gather_words([2], "gw2")
+        gather_scales([3], "gs3")
+        gather_words([3], "gw3")
+        gather_scales([4], "gs4")
+        gather_words([4], "gw4")
+        block(0, 0, "x0")
+        block(0, 1)
+        block(1, 0, "x1")
+        regroup(0)
         quantize(0)
-        layer2(0)
-        layer1(2)
-        gather_scales(3)
-        gather_words(3)
+        layer2(0, [0], "x0")
+        block(1, 1)
+        block(2, 0, "x2")
+        regroup(1)
         quantize(1)
-        layer2(1)
-        layer1(3)
-        gather_scales(4)
-        gather_words(4)
-        gather_scales(5)
-        gather_words(5)
-        scatter(0, 0)
+        evac(0, 0, 1)
+        scatter(0, 0, 256, 0)
+        block(2, 1)
+        block(3, 0, "x3")
+        regroup(2)
         quantize(2)
-        layer2(2)
-        layer1(4)
-        scatter(0, 1)
-        scatter(1, 0)
+        layer2(0, [1], "x2")
+        block(3, 1)
+        gather_scales([5], "gs3")
+        gather_words([5], "gw3")
+        evac(0, 1, 2)
+        scatter(0, 0, 256, 1)
+        block(4, 0, "x1")
+        regroup(3)
         quantize(3)
-        layer2(3)
-        layer1(5)
-        scatter(1, 1)
-        scatter(2, 0)
+        layer2(1, [0, 1], "x3")
+        block(4, 1)
+        evac(1, 0, 2)
+        scatter(0, 256, 512, 0)
+        scatter(0, 256, 512, 1)
+        block(5, 0, "x2")
+        regroup(4)
         quantize(4)
-        layer2(4)
-        scatter(3, 0)
+        layer2(2, [0, 1], "x1")
+        block(5, 1)
+        evac(2, 0, 2)
+        scatter(1, 0, 256, 0)
+        layer2(3, [0, 1], "x0")
+        evac(3, 0, 2)
+        scatter(0, 512, 768, 0)
+        regroup(5)
         quantize(5)
-        layer2(5)
-        scatter(2, 1)
-        scatter(4, 0)
-        scatter(5, 0)
-        scatter(3, 1)
-        finish(0, 1)
-        scatter(4, 1)
-        scatter(5, 1)
-        finish(1, 2)
+        layer2(4, [0], "x2")
+        evac(4, 0, 1)
+        scatter(0, 768, 1024, 0)
+        layer2(5, [0, 1], "x3")
+        evac(5, 0, 1)
+        scatter(1, 256, 512, 0)
+        evac(5, 1, 2)
+        scatter(1, 0, 512, 1)
+        layer2(4, [1], "x3")
+        evac(4, 1, 2)
+        scatter(0, 512, 1024, 1)
+        finish_on_tensor(0)
+        finish(1, [0, 512, 768, 1024])

@@ -36,7 +36,7 @@ def tile_moe_ada_mlp_relu_kernel(
         xw = keep.tile([P, T], I32, name="xw", align_bytes=64)
         w1s = keep.tile([P, H], U8, name="w1s", align_bytes=64)
         w2s = keep.tile([P, N], U8, name="w2s", align_bytes=64)
-        w1 = [keep.tile([P, H], I32, name="w1_%d" % e, align_bytes=64) for e in range(E)]
+        w1 = keep.tile([P, E, H], I32, name="w1", align_bytes=64)
         w2 = keep.tile([P, E, N], I32, name="w2", align_bytes=64)
         gates = [keep.tile([P, slots[c]], F32, name="gate%d" % c) for c in range(2)]
         ident = keep.tile([P, P], F32, name="ident")
@@ -44,65 +44,82 @@ def tile_moe_ada_mlp_relu_kernel(
         total = [keep.tile([P, T], F32, name="total%d" % a) for a in range(2)]
         ysb = [keep.tile([P, 2, slots[c]], F32, name="ysb%d" % c) for c in range(2)]
 
-        nc.vector.memset(w1s[:].bitcast(I32), 0)
-        nc.vector.memset(w2s[:].bitcast(I32), 0)
-        nc.sync.dma_start(lists[0][:], offs)
-        for q in range(4):
-            rows = x_scales[0, 4 * q : 4 * q + 4, :].bitcast(I32)
-            nc.sync.dma_start(xs[32 * q : 32 * q + 32, :].bitcast(I32), rows.unsqueeze(0).to_broadcast([8, 4, T // 4]))
-        nc.sync.dma_start(xw[:], x_words[0].rearrange("p t d -> p (t d)").bitcast(I32))
+        def load_scales(queue, plane, rows, q):
+            queue.dma_start(plane[32 * q : 32 * q + 16, :].bitcast(I32), rows[:, 0, 4 * q : 4 * q + 4, :].bitcast(I32))
+
+        def load_w1(e0, e1):
+            nc.sync.dma_start(w1[:, e0:e1, :], w1_words[e0:e1, 0].rearrange("e p i d -> p e (i d)").bitcast(I32))
+
+        nc.gpsimd.memset(xs[:].bitcast(I32), 0)
+        nc.gpsimd.memset(w1s[:].bitcast(I32), 0)
+        zero = keep.tile([P, 1], F32, name="zero")
+        nc.gpsimd.memset(zero[:], 0.0)
+        nc.gpsimd.memset(w2s[:].bitcast(I32), 0)
         make_identity(nc, ident[:])
 
-        def load_w1(e):
-            nc.sync.dma_start(w1[e][:], w1_words[e, 0].rearrange("p i d -> p (i d)").bitcast(I32))
+        def load_w2(queue, e0, e1):
+            queue.dma_start(w2[:, e0:e1, :], w2_words[e0:e1, 0].rearrange("e p n d -> p e (n d)").bitcast(I32))
 
-        load_w1(0)
-        for q in range(4):
-            nc.sync.dma_start(w1s[32 * q : 32 * q + 16, :].bitcast(I32), w1_scales[:, 0, 4 * q : 4 * q + 4, :].bitcast(I32))
+        def load_token_scales(q):
+            nc.sync.dma_start(xs[32 * q : 32 * q + 4, :].bitcast(I32), x_scales[0, 4 * q : 4 * q + 4, :].bitcast(I32))
+
+        load_token_scales(2)
+        load_token_scales(1)
+        nc.sync.dma_start(lists[0][:], offs)
+        load_token_scales(0)
+        load_token_scales(3)
+        nc.sync.dma_start(xw[:], x_words[0].rearrange("p t d -> p (t d)").bitcast(I32))
+        load_scales(nc.sync, w1s, w1_scales, 2)
+        load_w1(1, 2)
+        load_w1(0, 1)
         nc.sync.dma_start(lists[1][:], offs2)
-        load_w1(1)
-        for q in range(4):
-            nc.sync.dma_start(w2s[32 * q : 32 * q + 16, :].bitcast(I32), w2_scales[:, 0, 4 * q : 4 * q + 4, :].bitcast(I32))
-        nc.sync.dma_start(w2[:], w2_words[:, 0].rearrange("e p n d -> p e (n d)").bitcast(I32))
-        nc.sync.dma_start(gates[0][:], gate1)
-        load_w1(2)
-        load_w1(3)
-        nc.sync.dma_start(gates[1][:], gate2)
+        load_scales(nc.sync, w1s, w1_scales, 3)
+        load_scales(nc.sync, w1s, w1_scales, 0)
+        load_scales(nc.sync, w1s, w1_scales, 1)
+        load_w1(2, 3)
+        load_scales(nc.sync, w2s, w2_scales, 0)
+        load_scales(nc.sync, w2s, w2_scales, 2)
+        load_scales(nc.sync, w2s, w2_scales, 1)
+        load_w2(nc.sync, 0, 2)
+        load_scales(nc.sync, w2s, w2_scales, 3)
+        load_w2(nc.sync, 2, 4)
+        nc.sync.dma_start(gates[0][:, 0:512], gate1[:, 0:512])
+        load_w1(3, 4)
+        nc.sync.dma_start(gates[1][:, 0:512], gate2[:, 0:512])
+        nc.sync.dma_start(gates[0][:, 512:1024], gate1[:, 512:1024])
         for a in range(2):
-            nc.vector.memset(windows[1][a][:], 0.0)
+            nc.scalar.copy(windows[1][a][:], zero[:].to_broadcast([P, T]))
 
-        units = [(0, 0, (0, 0)), (0, 256, (1, 1)), (1, 0, (0, 1)), (0, 512, (2, 2)), (0, 768, (3, 3)), (1, 256, (2, 3))]
+        units = [(0, 0, (0,)), (0, 128, (0,)), (0, 256, (1, 1)), (0, 512, (2, 2)), (1, 0, (0, 1)), (0, 768, (3, 3)), (1, 256, (2, 3))]
 
         def offsets(c, s0, s1):
             return lists[c][:, s0 // 16 : s1 // 16]
 
         gw, gs = {}, {}
 
-        def gather_scales(us, tag):
-            c, s0 = units[us[0]][0], units[us[0]][1]
-            tile = keep.tile([P, U * len(us)], U8, name=tag, align_bytes=64)
-            nc.vector.tensor_copy(tile[:], xs[:].indirect(offsets(c, s0, s0 + U * len(us))))
-            for j, u in enumerate(us):
-                gs[u] = tile[:, j * U : (j + 1) * U]
+        def gather_scales(c, s0, tag):
+            tile = keep.tile([P, U], U8, name=tag, align_bytes=64)
+            nc.vector.tensor_copy(tile[:], xs[:].indirect(offsets(c, s0, s0 + U)))
+            for j in range(2):
+                gs[c, s0 + j * P] = tile[:, j * P : (j + 1) * P]
 
-        def gather_words(us, tag):
-            c, s0 = units[us[0]][0], units[us[0]][1]
-            tile = keep.tile([P, U * len(us)], I32, name=tag, align_bytes=64)
-            nc.vector.tensor_copy(tile[:].bitcast(U32), xw[:].bitcast(U32).indirect(offsets(c, s0, s0 + U * len(us))))
-            for j, u in enumerate(us):
-                gw[u] = tile[:, j * U : (j + 1) * U]
+        def gather_words(c, s0, tag):
+            tile = keep.tile([P, U], I32, name=tag, align_bytes=64)
+            nc.vector.tensor_copy(tile[:].bitcast(U32), xw[:].bitcast(U32).indirect(offsets(c, s0, s0 + U)))
+            for j in range(2):
+                gw[c, s0 + j * P] = tile[:, j * P : (j + 1) * P]
 
         hin, turned = {}, {}
 
-        def block(u, b, bank=None):
-            e = units[u][2][b]
+        def block(u, b, sums_bank, bank=None):
+            c, s0, experts = units[u]
+            e = experts[b]
             if b == 0:
-                turned[u] = psum.tile([P, 2, 2, P], F32, name=bank, bufs=1)
-            cols = slice(b * P, (b + 1) * P)
-            acc = psum.tile([P, H], F32, name="acc1", bufs=4)
+                turned[u] = psum.tile([P, len(experts), 2, P], F32, name=bank, bufs=1)
+            acc = psum.tile([P, H], F32, name=sums_bank, bufs=1)
             nc.tensor.matmul_mx(
-                out=acc[:], lhsT=gw[u][:, cols].bitcast(FP8X4), lhsT_scale=gs[u][:, cols],
-                rhs=w1[e][:].bitcast(FP8X4), rhs_scale=w1s[4 * e : P, :], start=True, stop=True,
+                out=acc[:], lhsT=gw[c, s0 + b * P].bitcast(FP8X4), lhsT_scale=gs[c, s0 + b * P],
+                rhs=w1[:, e, :].bitcast(FP8X4), rhs_scale=w1s[4 * e : P, :], start=True, stop=True,
             )
             hb = ring.tile([P, H], BF16, name="hb", bufs=4)
             nc.scalar.activation(
@@ -114,17 +131,19 @@ def tile_moe_ada_mlp_relu_kernel(
                 nc.tensor.transpose(turned[u][:, b, v, :], hb[:].bitcast(F32)[:, v * P : (v + 1) * P], ident[:])
 
         def regroup(u):
-            hin[u] = keep.tile([P, 4 * U], BF16, name="hin%d" % u, align_bytes=64)
+            blocks = len(units[u][2])
+            hin[u] = keep.tile([P, 4 * P * blocks], BF16, name="hin%d" % u, align_bytes=64)
             nc.scalar.copy(
-                hin[u][:].bitcast(F32).rearrange("p (b s v) -> p b s v", b=2, v=2),
+                hin[u][:].bitcast(F32).rearrange("p (b s v) -> p b s v", b=blocks, v=2),
                 turned[u][:].rearrange("p b v s -> p b s v"),
             )
 
         hq = {}
 
         def quantize(u):
-            words = keep.tile([P, U], U32, name="hw%d" % u, align_bytes=64)
-            scales = keep.tile([P, U], U8, name="hs%d" % u, align_bytes=64)
+            width = P * len(units[u][2])
+            words = keep.tile([P, width], U32, name="hw%d" % u, align_bytes=64)
+            scales = keep.tile([P, width], U8, name="hs%d" % u, align_bytes=64)
             nc.vector.quantize_mx(out=words[:].bitcast(FP8X4), scales=scales[:], in_=hin[u][:])
             hq[u] = (words, scales)
 
@@ -132,9 +151,10 @@ def tile_moe_ada_mlp_relu_kernel(
 
         def layer2(u, halves, bank):
             experts = units[u][2]
+            width = P * len(experts)
             words, scales = hq[u]
-            acc = psum.tile([P, 2, U], F32, name=bank, bufs=1)
-            runs = [(experts[0], slice(0, U))] if experts[0] == experts[1] else [(experts[b], slice(b * P, (b + 1) * P)) for b in range(2)]
+            acc = psum.tile([P, 2, width], F32, name=bank, bufs=1)
+            runs = [(experts[0], slice(0, width))] if experts[0] == experts[-1] else [(experts[b], slice(b * P, (b + 1) * P)) for b in range(2)]
             for a in halves:
                 acc2[u, a] = acc
                 ncols = slice(a * P, (a + 1) * P)
@@ -145,8 +165,8 @@ def tile_moe_ada_mlp_relu_kernel(
                     )
 
         def evac(u, a0, a1):
-            c, s0 = units[u][0], units[u][1]
-            nc.scalar.copy(ysb[c][:, a0:a1, s0 : s0 + U], acc2[u, a0][:, a0:a1, :])
+            c, s0, experts = units[u]
+            nc.scalar.copy(ysb[c][:, a0:a1, s0 : s0 + P * len(experts)], acc2[u, a0][:, a0:a1, :])
 
         def scatter(c, s0, s1, a):
             nc.vector.tensor_tensor(windows[c][a][:].indirect(offsets(c, s0, s1)), ysb[c][:, a, s0:s1], gates[c][:, s0:s1], MULT)
@@ -159,81 +179,88 @@ def tile_moe_ada_mlp_relu_kernel(
 
         def finish_on_tensor(a):
             for half in range(2):
-                summed = psum.tile([P, 4, P], F32, name="acc1", bufs=4)
+                summed = psum.tile([P, 4, P], F32, name=("b0", "b2")[half], bufs=1)
                 for j in range(4):
                     cols = slice((4 * half + j) * P, (4 * half + j + 1) * P)
                     for c in range(2):
                         nc.tensor.matmul(summed[:, j, :], lhsT=windows[c][a][:, cols], rhs=ident[:], start=(c == 0), stop=(c == 1), is_transpose=True)
                 flipped = ring.tile([P, 4, P], F32, name="flipped")
                 nc.scalar.copy(flipped[:], summed[:])
-                back = psum.tile([P, 4, P], F32, name="acc1", bufs=4)
+                back = psum.tile([P, 4, P], F32, name=("b4", "b5")[half], bufs=1)
                 for j in range(4):
                     nc.tensor.transpose(back[:, j, :], flipped[:, j, :], ident[:])
                 cols = slice(half * 4 * P, (half + 1) * 4 * P)
                 nc.scalar.copy(total[a][:, cols], back[:].rearrange("p j t -> p (j t)"))
-                nc.sync.dma_start(out[a * P : (a + 1) * P, cols], total[a][:, cols])
+                nc.scalar.dma_start(out[a * P : (a + 1) * P, cols], total[a][:, cols])
 
-        gather_scales([0, 1], "gs01")
-        gather_words([0], "gw0")
-        gather_words([1], "gw1")
-        gather_scales([2], "gs2")
-        gather_words([2], "gw2")
-        gather_scales([3], "gs3")
-        gather_words([3], "gw3")
-        gather_scales([4], "gs4")
-        gather_words([4], "gw4")
-        block(0, 0, "x0")
-        block(0, 1)
-        block(1, 0, "x1")
+        gather_words(0, 0, "gwb")
+        gather_scales(0, 0, "gsc")
+        block(0, 0, "b2", "b7")
         regroup(0)
         quantize(0)
-        layer2(0, [0], "x0")
-        block(1, 1)
-        block(2, 0, "x2")
+        gather_scales(0, 256, "gsd")
+        layer2(0, [0, 1], "b2")
+        evac(0, 0, 2)
+        gather_scales(1, 0, "gse")
+        gather_words(0, 256, "gwd")
+        block(2, 0, "b6", "b0")
+        gather_words(0, 768, "gwe")
+        gather_words(0, 512, "gwa")
+        block(1, 0, "b1", "b3")
+        gather_scales(0, 512, "gsa")
         regroup(1)
+        block(2, 1, "b6")
         quantize(1)
-        evac(0, 0, 1)
-        scatter(0, 0, 256, 0)
-        block(2, 1)
-        block(3, 0, "x3")
+        gather_words(1, 0, "gwd")
+        layer2(1, [0, 1], "b5")
+        gather_scales(1, 256, "gsd")
+        evac(1, 0, 2)
+        block(3, 0, "b1", "b2")
+        block(3, 1, "b3")
         regroup(2)
         quantize(2)
-        layer2(0, [1], "x2")
-        block(3, 1)
-        gather_scales([5], "gs3")
-        gather_words([5], "gw3")
-        evac(0, 1, 2)
-        scatter(0, 0, 256, 1)
-        block(4, 0, "x1")
         regroup(3)
+        block(4, 0, "b1", "b6")
         quantize(3)
-        layer2(1, [0, 1], "x3")
-        block(4, 1)
-        evac(1, 0, 2)
-        scatter(0, 256, 512, 0)
-        scatter(0, 256, 512, 1)
-        block(5, 0, "x2")
+        layer2(2, [0], "b1")
+        block(4, 1, "b5")
+        gather_scales(0, 768, "gsc")
+        scatter(0, 0, 128, 1)
+        gather_words(1, 256, "gwf")
+        evac(2, 0, 1)
+        scatter(0, 0, 128, 0)
+        layer2(3, [0, 1], "b7")
         regroup(4)
+        block(5, 0, "b4", "b6")
         quantize(4)
-        layer2(2, [0, 1], "x1")
-        block(5, 1)
-        evac(2, 0, 2)
-        scatter(1, 0, 256, 0)
-        layer2(3, [0, 1], "x0")
+        scatter(0, 128, 256, 0)
+        block(5, 1, "b2")
         evac(3, 0, 2)
+        scatter(0, 256, 512, 0)
+        block(6, 0, "b0", "b7")
+        layer2(2, [1], "b5")
+        block(6, 1, "b4")
         scatter(0, 512, 768, 0)
+        regroup(6)
+        evac(2, 1, 2)
         regroup(5)
+        quantize(6)
+        layer2(4, [0, 1], "b5")
         quantize(5)
-        layer2(4, [0], "x2")
-        evac(4, 0, 1)
-        scatter(0, 768, 1024, 0)
-        layer2(5, [0, 1], "x3")
+        layer2(5, [0], "b2")
+        evac(4, 0, 2)
+        layer2(6, [0, 1], "b0")
         evac(5, 0, 1)
-        scatter(1, 256, 512, 0)
+        scatter(0, 768, 1024, 0)
+        layer2(5, [1], "b2")
         evac(5, 1, 2)
+        scatter(0, 128, 256, 1)
+        scatter(0, 256, 512, 1)
+        evac(6, 0, 1)
+        scatter(1, 0, 256, 0)
+        evac(6, 1, 2)
         scatter(1, 0, 512, 1)
-        layer2(4, [1], "x3")
-        evac(4, 1, 2)
         scatter(0, 512, 1024, 1)
+        scatter(1, 256, 512, 0)
         finish_on_tensor(0)
-        finish(1, [0, 512, 768, 1024])
+        finish(1, [0, 512, 1024])

from contextlib import ExitStack

import concourse.mybir as mybir
from concourse.masks import make_identity

K, T, E, C, D, H, N = 512, 1024, 4, 256, 128, 512, 256
FLOPS = 2 * (E * C + E * D) * (K * H + H * N)

F32 = mybir.dt.float32
BF16 = mybir.dt.bfloat16
I32 = mybir.dt.int32
U32 = mybir.dt.uint32
U16 = mybir.dt.uint16
U8 = mybir.dt.uint8
FP8X4 = mybir.dt.float8_e4m3fn_x4
RELU = mybir.ActivationFunctionType.Relu
MULT = mybir.AluOpType.mult
ADD = mybir.AluOpType.add

P = 128
U = 256


def tile_moe_ada_mlp_relu_kernel(
    tc, x_words, x_scales, w1_words, w1_scales, w2_words, w2_scales, gate1, gate2, offs, offs2, out
):
    nc = tc.nc
    with ExitStack() as ctx:
        keep = ctx.enter_context(tc.tile_pool(name="keep", bufs=1))
        ring = ctx.enter_context(tc.tile_pool(name="ring", bufs=3))
        psum = ctx.enter_context(tc.psum_pool(name="psum", bufs=1))

        slots = (E * C, E * D)
        lists = [keep.tile([P, slots[c] // 16], U16, name="list%d" % c) for c in range(2)]
        xs = keep.tile([P, T], U8, name="xs", align_bytes=64)
        xw = keep.tile([P, T], I32, name="xw", align_bytes=64)
        w1s = keep.tile([P, H], U8, name="w1s", align_bytes=64)
        w2s = keep.tile([P, N], U8, name="w2s", align_bytes=64)
        w1 = keep.tile([P, E, H], I32, name="w1", align_bytes=64)
        w2 = keep.tile([P, E, N], I32, name="w2", align_bytes=64)
        gates = [keep.tile([P, slots[c]], F32, name="gate%d" % c) for c in range(2)]
        ident = keep.tile([P, P], F32, name="ident")
        windows = [[keep.tile([P, T], F32, name="window%d%d" % (c, a)) for a in range(2)] for c in range(2)]
        total = [keep.tile([P, T], F32, name="total%d" % a) for a in range(2)]
        ysb = [keep.tile([P, 2, slots[c]], F32, name="ysb%d" % c) for c in range(2)]

        def load_scales(queue, plane, rows, q):
            queue.dma_start(plane[32 * q : 32 * q + 16, :].bitcast(I32), rows[:, 0, 4 * q : 4 * q + 4, :].bitcast(I32))

        def load_w1(e0, e1):
            nc.sync.dma_start(w1[:, e0:e1, :], w1_words[e0:e1, 0].rearrange("e p i d -> p e (i d)").bitcast(I32))

        nc.gpsimd.memset(xs[:].bitcast(I32), 0)
        nc.gpsimd.memset(w1s[:].bitcast(I32), 0)
        zero = keep.tile([P, 1], F32, name="zero")
        nc.gpsimd.memset(zero[:], 0.0)
        nc.gpsimd.memset(w2s[:].bitcast(I32), 0)
        make_identity(nc, ident[:])

        def load_w2(queue, e0, e1):
            queue.dma_start(w2[:, e0:e1, :], w2_words[e0:e1, 0].rearrange("e p n d -> p e (n d)").bitcast(I32))

        def load_token_scales(q):
            nc.sync.dma_start(xs[32 * q : 32 * q + 4, :].bitcast(I32), x_scales[0, 4 * q : 4 * q + 4, :].bitcast(I32))

        load_token_scales(2)
        load_token_scales(1)
        nc.sync.dma_start(lists[0][:], offs)
        load_token_scales(0)
        load_token_scales(3)
        nc.sync.dma_start(xw[:], x_words[0].rearrange("p t d -> p (t d)").bitcast(I32))
        load_scales(nc.sync, w1s, w1_scales, 2)
        load_w1(1, 2)
        load_w1(0, 1)
        nc.sync.dma_start(lists[1][:], offs2)
        load_scales(nc.sync, w1s, w1_scales, 3)
        load_scales(nc.sync, w1s, w1_scales, 0)
        load_scales(nc.sync, w1s, w1_scales, 1)
        load_w1(2, 3)
        load_scales(nc.sync, w2s, w2_scales, 0)
        load_scales(nc.sync, w2s, w2_scales, 2)
        load_scales(nc.sync, w2s, w2_scales, 1)
        load_w2(nc.sync, 0, 2)
        load_scales(nc.sync, w2s, w2_scales, 3)
        load_w2(nc.sync, 2, 4)
        nc.sync.dma_start(gates[0][:, 0:512], gate1[:, 0:512])
        load_w1(3, 4)
        nc.sync.dma_start(gates[1][:, 0:512], gate2[:, 0:512])
        nc.sync.dma_start(gates[0][:, 512:1024], gate1[:, 512:1024])
        for a in range(2):
            nc.scalar.copy(windows[1][a][:], zero[:].to_broadcast([P, T]))

        units = [(0, 0, (0,)), (0, 128, (0,)), (0, 256, (1, 1)), (0, 512, (2, 2)), (1, 0, (0, 1)), (0, 768, (3, 3)), (1, 256, (2, 3))]

        def offsets(c, s0, s1):
            return lists[c][:, s0 // 16 : s1 // 16]

        gw, gs = {}, {}

        def gather_scales(c, s0, tag):
            tile = keep.tile([P, U], U8, name=tag, align_bytes=64)
            nc.vector.tensor_copy(tile[:], xs[:].indirect(offsets(c, s0, s0 + U)))
            for j in range(2):
                gs[c, s0 + j * P] = tile[:, j * P : (j + 1) * P]

        def gather_words(c, s0, tag):
            tile = keep.tile([P, U], I32, name=tag, align_bytes=64)
            nc.vector.tensor_copy(tile[:].bitcast(U32), xw[:].bitcast(U32).indirect(offsets(c, s0, s0 + U)))
            for j in range(2):
                gw[c, s0 + j * P] = tile[:, j * P : (j + 1) * P]

        hin, turned = {}, {}

        def block(u, b, sums_bank, bank=None):
            c, s0, experts = units[u]
            e = experts[b]
            if b == 0:
                turned[u] = psum.tile([P, len(experts), 2, P], F32, name=bank, bufs=1)
            acc = psum.tile([P, H], F32, name=sums_bank, bufs=1)
            nc.tensor.matmul_mx(
                out=acc[:], lhsT=gw[c, s0 + b * P].bitcast(FP8X4), lhsT_scale=gs[c, s0 + b * P],
                rhs=w1[:, e, :].bitcast(FP8X4), rhs_scale=w1s[4 * e : P, :], start=True, stop=True,
            )
            hb = ring.tile([P, H], BF16, name="hb", bufs=4)
            nc.scalar.activation(
                hb[:].rearrange("s (v p d) -> s v p d", v=2, d=2),
                acc[:].rearrange("s (p v d) -> s v p d", v=2, d=2),
                RELU,
            )
            for v in range(2):
                nc.tensor.transpose(turned[u][:, b, v, :], hb[:].bitcast(F32)[:, v * P : (v + 1) * P], ident[:])

        def regroup(u):
            blocks = len(units[u][2])
            hin[u] = keep.tile([P, 4 * P * blocks], BF16, name="hin%d" % u, align_bytes=64)
            nc.scalar.copy(
                hin[u][:].bitcast(F32).rearrange("p (b s v) -> p b s v", b=blocks, v=2),
                turned[u][:].rearrange("p b v s -> p b s v"),
            )

        hq = {}

        def quantize(u):
            width = P * len(units[u][2])
            words = keep.tile([P, width], U32, name="hw%d" % u, align_bytes=64)
            scales = keep.tile([P, width], U8, name="hs%d" % u, align_bytes=64)
            nc.vector.quantize_mx(out=words[:].bitcast(FP8X4), scales=scales[:], in_=hin[u][:])
            hq[u] = (words, scales)

        acc2 = {}

        def layer2(u, halves, bank):
            experts = units[u][2]
            width = P * len(experts)
            words, scales = hq[u]
            acc = psum.tile([P, 2, width], F32, name=bank, bufs=1)
            runs = [(experts[0], slice(0, width))] if experts[0] == experts[-1] else [(experts[b], slice(b * P, (b + 1) * P)) for b in range(2)]
            for a in halves:
                acc2[u, a] = acc
                ncols = slice(a * P, (a + 1) * P)
                for e, cols in runs:
                    nc.tensor.matmul_mx(
                        out=acc[:, a, cols], lhsT=w2[:, e, ncols].bitcast(FP8X4), lhsT_scale=w2s[4 * e : P, ncols],
                        rhs=words[:, cols].bitcast(FP8X4), rhs_scale=scales[:, cols], start=True, stop=True,
                    )

        def evac(u, a0, a1):
            c, s0, experts = units[u]
            nc.scalar.copy(ysb[c][:, a0:a1, s0 : s0 + P * len(experts)], acc2[u, a0][:, a0:a1, :])

        def scatter(c, s0, s1, a):
            nc.vector.tensor_tensor(windows[c][a][:].indirect(offsets(c, s0, s1)), ysb[c][:, a, s0:s1], gates[c][:, s0:s1], MULT)

        def finish(a, cuts):
            for j in range(len(cuts) - 1):
                cols = slice(cuts[j], cuts[j + 1])
                nc.vector.tensor_tensor(total[a][:, cols], windows[0][a][:, cols], windows[1][a][:, cols], ADD)
                nc.sync.dma_start(out[a * P : (a + 1) * P, cols], total[a][:, cols])

        def finish_on_tensor(a):
            for half in range(2):
                summed = psum.tile([P, 4, P], F32, name=("b0", "b2")[half], bufs=1)
                for j in range(4):
                    cols = slice((4 * half + j) * P, (4 * half + j + 1) * P)
                    for c in range(2):
                        nc.tensor.matmul(summed[:, j, :], lhsT=windows[c][a][:, cols], rhs=ident[:], start=(c == 0), stop=(c == 1), is_transpose=True)
                flipped = ring.tile([P, 4, P], F32, name="flipped")
                nc.scalar.copy(flipped[:], summed[:])
                back = psum.tile([P, 4, P], F32, name=("b4", "b5")[half], bufs=1)
                for j in range(4):
                    nc.tensor.transpose(back[:, j, :], flipped[:, j, :], ident[:])
                cols = slice(half * 4 * P, (half + 1) * 4 * P)
                nc.scalar.copy(total[a][:, cols], back[:].rearrange("p j t -> p (j t)"))
                nc.scalar.dma_start(out[a * P : (a + 1) * P, cols], total[a][:, cols])

        gather_words(0, 0, "gwb")
        gather_scales(0, 0, "gsc")
        block(0, 0, "b2", "b7")
        regroup(0)
        quantize(0)
        gather_scales(0, 256, "gsd")
        layer2(0, [0, 1], "b2")
        evac(0, 0, 2)
        gather_scales(1, 0, "gse")
        gather_words(0, 256, "gwd")
        block(2, 0, "b6", "b0")
        gather_words(0, 768, "gwe")
        gather_words(0, 512, "gwa")
        block(1, 0, "b1", "b3")
        gather_scales(0, 512, "gsa")
        regroup(1)
        block(2, 1, "b6")
        quantize(1)
        gather_words(1, 0, "gwd")
        layer2(1, [0, 1], "b5")
        gather_scales(1, 256, "gsd")
        evac(1, 0, 2)
        block(3, 0, "b1", "b2")
        block(3, 1, "b3")
        regroup(2)
        quantize(2)
        regroup(3)
        block(4, 0, "b1", "b6")
        quantize(3)
        layer2(2, [0], "b1")
        block(4, 1, "b5")
        gather_scales(0, 768, "gsc")
        scatter(0, 0, 128, 1)
        gather_words(1, 256, "gwf")
        evac(2, 0, 1)
        scatter(0, 0, 128, 0)
        layer2(3, [0, 1], "b7")
        regroup(4)
        block(5, 0, "b4", "b6")
        quantize(4)
        scatter(0, 128, 256, 0)
        block(5, 1, "b2")
        evac(3, 0, 2)
        scatter(0, 256, 512, 0)
        block(6, 0, "b0", "b7")
        layer2(2, [1], "b5")
        block(6, 1, "b4")
        scatter(0, 512, 768, 0)
        regroup(6)
        evac(2, 1, 2)
        regroup(5)
        quantize(6)
        layer2(4, [0, 1], "b5")
        quantize(5)
        layer2(5, [0], "b2")
        evac(4, 0, 2)
        layer2(6, [0, 1], "b0")
        evac(5, 0, 1)
        scatter(0, 768, 1024, 0)
        layer2(5, [1], "b2")
        evac(5, 1, 2)
        scatter(0, 128, 256, 1)
        scatter(0, 256, 512, 1)
        evac(6, 0, 1)
        scatter(1, 0, 256, 0)
        evac(6, 1, 2)
        scatter(1, 0, 512, 1)
        scatter(0, 512, 1024, 1)
        scatter(1, 256, 512, 0)
        finish_on_tensor(0)
        finish(1, [0, 512, 1024])
